import numpy as np
import ml_dtypes


def mxq(x, axis, fmt="e4m3"):
    dtype, down = {"e4m3": (ml_dtypes.float8_e4m3fn, 7), "e5m2": (ml_dtypes.float8_e5m2, 14)}[fmt]
    v = np.moveaxis(np.asarray(x, np.float32).astype(ml_dtypes.bfloat16).astype(np.float64), axis, -1)
    blocks = v.reshape(v.shape[:-1] + (-1, 32))
    amax = np.abs(blocks).max(-1, keepdims=True)
    byte = np.maximum(np.where(amax > 0, np.frexp(amax)[1] - 1 + 127, 0) - down, 1)
    scale = np.exp2(byte - 127.0)
    codes = (blocks / scale).astype(np.float32).astype(dtype).astype(np.float64)
    return np.moveaxis((codes * scale).reshape(v.shape), -1, axis)


WIDE = False


def mx_kscale(k):
    if not WIDE:
        return np.ones(k)
    levels = np.array([10, -10, 5, -5, 0])
    if k % 512:
        return np.exp2(np.random.permutation(np.resize(levels, k // 32))).repeat(32)
    a = np.empty((k // 512, 16))
    for p in range(k // 512):
        a[p, :8] = np.random.permutation(np.resize(levels, 8))
        for g in range(8):
            far = levels[np.abs(levels - a[p, g]) >= 10]
            a[p, g + 8] = far[np.random.randint(len(far))]
    return np.exp2(a.ravel()).repeat(32)


BF16 = ml_dtypes.bfloat16


def bf(x):
    return np.asarray(x, np.float32).astype(BF16)


def f64(x):
    return np.asarray(x).astype(np.float64)


E2M1 = np.array([0.0, 0.5, 1.0, 1.5, 2.0, 3.0, 4.0, 6.0, -0.0, -0.5, -1.0, -1.5, -2.0, -3.0, -4.0, -6.0])


def pack_weight(w, fmt):
    k, n = w.shape
    w = f64(bf(w)).reshape(k // 32, 32, n)
    amax = np.abs(w).max(1)
    if fmt == "e4m3":
        byte = np.frexp(amax)[1] - 1 + 127 - 7
    else:
        mant, ex = np.frexp(amax / 6.0)
        byte = np.where(mant > 0.5, ex, ex - 1) + 127
    byte = np.clip(np.where(amax > 0, byte, 1), 1, 254)
    scaled = (w * np.exp2(127.0 - byte)[:, None, :]).reshape(k, n).astype(np.float32)
    by_word = np.ascontiguousarray(scaled.reshape(k // 512, 128, 4, n).transpose(0, 1, 3, 2))
    if fmt == "e4m3":
        words = by_word.astype(ml_dtypes.float8_e4m3fn).view(np.uint8)
    else:
        c = by_word.astype(ml_dtypes.float4_e2m1fn).view(np.uint8) & 0xF
        words = c[..., 0::2] | (c[..., 1::2] << 4)
    return np.ascontiguousarray(words), np.ascontiguousarray(byte.astype(np.uint8).reshape(k // 512, 16, n))


def unpack_weight(words, scales, fmt):
    g, p, n, _ = words.shape
    if fmt == "e4m3":
        vals = np.ascontiguousarray(words).view(ml_dtypes.float8_e4m3fn).astype(np.float64)
    else:
        nib = np.empty((g, p, n, 4), np.uint8)
        nib[..., 0::2] = words & 0xF
        nib[..., 1::2] = words >> 4
        vals = E2M1[nib]
    vals = vals * np.repeat(np.exp2(scales.astype(np.float64) - 127.0), 8, axis=1)[..., None]
    return vals.transpose(0, 1, 3, 2).reshape(g * 512, n)


B, S, R, D, E, T = 2, 1024, 1024, 512, 512, 2


def draw0():
    s, t = mx_kscale(S), mx_kscale(D)
    x = bf(np.random.standard_normal((B, S, D)) * s[:, None])
    mp_words, mp_scales = pack_weight((np.random.standard_normal((R, S)) / np.sqrt(S) / s[None, :]).T, "e4m3")
    mq_words, mq_scales = pack_weight((np.random.standard_normal((R, S)) / np.sqrt(S) / s[None, :]).T, "e4m3")
    mr_words, mr_scales = pack_weight((np.random.standard_normal((R, S)) / np.sqrt(S) / s[None, :]).T, "e4m3")
    coef = bf(np.random.uniform(0.4, 1.0, (T, D)))
    gain = bf((1.0 + 0.1 * np.random.standard_normal(D)) * t)
    wo_words, wo_scales = pack_weight(np.random.standard_normal((D, E)) / np.sqrt(D) / t[:, None], "e4m3")
    return {
        "x": x,
        "mp_words": mp_words,
        "mp_scales": mp_scales,
        "mq_words": mq_words,
        "mq_scales": mq_scales,
        "mr_words": mr_words,
        "mr_scales": mr_scales,
        "coef": coef,
        "gain": gain,
        "wo_words": wo_words,
        "wo_scales": wo_scales,
    }


def mix_time(m_words, m_scales, xq):
    return unpack_weight(m_words, m_scales, "e4m3").T @ xq


def core(x, mp_words, mp_scales, mq_words, mq_scales, mr_words, mr_scales, coef, gain, wo_words, wo_scales):
    c = f64(coef)
    xq = mxq(f64(x), 1, "e4m3")
    p = mix_time(mp_words, mp_scales, xq)
    q = mix_time(mq_words, mq_scales, xq)
    r = mix_time(mr_words, mr_scales, xq)
    h = c[0] + c[1] * r
    y = p * (1.0 + q * h)
    z = y * f64(gain)
    return mxq(z, 2, "e4m3") @ unpack_weight(wo_words, wo_scales, "e4m3")


def e4m3fn_bytes(y):
    return np.clip(np.asarray(y, np.float64), -448.0, 448.0).astype(np.float32).astype(ml_dtypes.float8_e4m3fn).view(np.uint8)


def e4m3fn_values(b):
    return np.asarray(b, np.uint8).view(ml_dtypes.float8_e4m3fn).astype(np.float64)


def setup_inputs():
    d = draw0()
    x0 = np.asarray(d['x']).astype(np.float64)
    s = (np.max(np.abs(x0), axis=(0, 2), keepdims=True) / 448.0).astype(np.float32)
    out = {}
    for k, v in d.items():
        if k == 'x':
            out['x_bytes'] = e4m3fn_bytes(x0 / s.astype(np.float64))
            out['x_scale'] = s
        else:
            out[k] = v
    return out


def reference(x_bytes, x_scale, mp_words, mp_scales, mq_words, mq_scales, mr_words, mr_scales, coef, gain, wo_words, wo_scales):
    return core(e4m3fn_values(x_bytes) * x_scale.astype(np.float64), mp_words, mp_scales, mq_words, mq_scales, mr_words, mr_scales, coef, gain, wo_words, wo_scales)

@@ -1,0 +1,308 @@
+from contextlib import ExitStack
+
+import concourse.mybir as mybir
+
+F32 = mybir.dt.float32
+BF16 = mybir.dt.bfloat16
+I32 = mybir.dt.int32
+U32 = mybir.dt.uint32
+U8 = mybir.dt.uint8
+FP8 = mybir.dt.float8_e4m3fn
+FP8X4 = mybir.dt.float8_e4m3fn_x4
+
+ALU = mybir.AluOpType
+ACT = mybir.ActivationFunctionType
+
+B, S, R, D, E = 2, 1024, 1024, 512, 512
+P = 128
+PACK = 4
+K_PASS = P * PACK
+GS = S // K_PASS
+BANK = 512
+
+FLOPS = 2 * B * R * S * D * 3 + 2 * B * R * D * E + 6 * B * R * D
+
+CHUNKS = [(0, 0, 512), (0, 512, 512), (1, 0, 512), (1, 512, 256), (1, 768, 128), (1, 896, 128)]
+
+
+def tile_volterrathirdordermixer_w8_kernel(
+    tc, x_bytes, x_scale, mp_words, mp_scales, mq_words, mq_scales, mr_words, mr_scales, coef, gain, wo_words, wo_scales, out
+):
+    nc = tc.nc
+    with ExitStack() as ctx:
+        keep = ctx.enter_context(tc.tile_pool(name="keep", bufs=1))
+        work = ctx.enter_context(tc.tile_pool(name="work", bufs=3))
+        psum = ctx.enter_context(tc.psum_pool(name="psum", bufs=2))
+        ctx.enter_context(tc.manual_schedule())
+
+        xb = [[keep.tile([P, PACK * D], U8, name="xb%d%d" % (b, g)) for g in range(GS)] for b in range(B)]
+        xs = keep.tile([P, GS, PACK], F32, name="xs")
+        xw = [keep.tile([P, GS, PACK, D], BF16, name="xw%d" % b) for b in range(B)]
+        xi = [keep.tile([P, PACK, GS, P * PACK], BF16, name="xi%d" % b, align_bytes=64) for b in range(B)]
+        xc = [keep.tile([P, PACK, GS, P], U32, name="xc%d" % b, align_bytes=64) for b in range(B)]
+        xsc = [keep.tile([P, PACK, GS, P], U8, name="xsc%d" % b, align_bytes=64) for b in range(B)]
+        planes = {w: keep.tile([P, R], U8, name="planes_" + w, align_bytes=64) for w in "rqp"}
+        codes = {(w, h): keep.tile([P, GS, BANK], U32, name="codes_%s%d" % (w, h), align_bytes=64) for w in "rqp" for h in range(2)}
+        wo_planes = keep.tile([P, E], U8, name="wo_planes", align_bytes=64)
+        wo_codes = keep.tile([P, E], U32, name="wo_codes", align_bytes=64)
+        coefs = keep.tile([P, 2, PACK], BF16, name="coefs")
+        gains = keep.tile([P, PACK], BF16, name="gains")
+        gc = keep.tile([P, 2, PACK], F32, name="gc")
+        gf = keep.tile([P, PACK], F32, name="gf")
+        warm = keep.tile([P, 8], F32, name="warm")
+
+        scales_in = {"r": mr_scales, "q": mq_scales, "p": mp_scales}
+        words_in = {"r": mr_words, "q": mq_words, "p": mp_words}
+
+        nc.gpsimd.dma_start(out=coefs[:], in_=coef.rearrange("c (p j) -> p c j", j=PACK))
+        nc.gpsimd.dma_start(out=gains[:], in_=gain.rearrange("(p j) -> p j", j=PACK))
+        nc.gpsimd.memset(warm[:], 0.0)
+        for w in "rqp":
+            nc.vector.memset(planes[w][:].bitcast(I32), 0)
+        nc.vector.memset(wo_planes[:].bitcast(I32), 0)
+
+        def load_x(b, g):
+            nc.sync.dma_start(out=xb[b][g][:], in_=x_bytes[b, g * K_PASS : (g + 1) * K_PASS, :].rearrange("(p t) d -> p (t d)", t=PACK))
+
+        def load_scales(w):
+            for quad in range(4):
+                nc.sync.dma_start(
+                    out=planes[w][32 * quad : 32 * quad + 8, :].bitcast(I32),
+                    in_=scales_in[w][:, 4 * quad : 4 * quad + 4, :].bitcast(I32),
+                )
+
+        def load_codes(w, h):
+            view = words_in[w].rearrange("g p n t -> p g (n t)")
+            nc.sync.dma_start(
+                out=codes[w, h][:].bitcast(I32), in_=view[:, :, h * BANK * PACK : (h + 1) * BANK * PACK].bitcast(I32)
+            )
+
+        nc.sync.dma_start(out=xs[:], in_=x_scale[0].rearrange("(g p t) o -> p g (t o)", g=GS, t=PACK))
+        load_x(0, 0)
+        load_x(0, 1)
+        load_scales("r")
+        load_codes("r", 0)
+        for w in "qp":
+            load_codes(w, 0)
+            load_scales(w)
+        load_x(1, 0)
+        load_x(1, 1)
+        for w in "rqp":
+            load_codes(w, 1)
+        for quad in range(4):
+            nc.sync.dma_start(
+                out=wo_planes[32 * quad : 32 * quad + 4, :].bitcast(I32), in_=wo_scales[0, 4 * quad : 4 * quad + 4, :].bitcast(I32)
+            )
+        nc.sync.dma_start(out=wo_codes[:].bitcast(I32), in_=wo_words[0].rearrange("p n t -> p (n t)").bitcast(I32))
+
+        def widen(b, g, t, on_scalar):
+            src = xb[b][g][:, t * D : (t + 1) * D].bitcast(FP8)
+            if on_scalar:
+                nc.scalar.activation(out=xw[b][:, g, t, :], in_=src, func=ACT.Copy, scale=xs[:, g, t : t + 1])
+            else:
+                nc.vector.tensor_scalar(out=xw[b][:, g, t, :], in0=src, scalar1=xs[:, g, t : t + 1], scalar2=None, op0=ALU.mult)
+
+        def copy(on_scalar, dst, src):
+            if on_scalar == "G":
+                nc.gpsimd.tensor_scalar(out=dst, in0=src, scalar1=1.0, scalar2=0.0, op0=ALU.mult, op1=ALU.add)
+            elif on_scalar:
+                nc.scalar.copy(out=dst, in_=src)
+            else:
+                nc.vector.tensor_copy(out=dst, in_=src)
+
+        def interleave_x(b, j, on_scalar, gs=None):
+            if gs is None:
+                src = xw[b][:].rearrange("p g t (m j) -> p j g m t", j=PACK)[:, j]
+                dst = xi[b][:, j].rearrange("p g (m t) -> p g m t", t=PACK)
+            else:
+                src = xw[b][:, gs].rearrange("p t (m j) -> p j m t", j=PACK)[:, j]
+                dst = xi[b][:, j, gs].rearrange("p (m t) -> p m t", t=PACK)
+            copy(on_scalar, dst, src)
+
+        def quantize_x(b, j, gs=None):
+            if gs is None:
+                nc.vector.quantize_mx(
+                    out=xc[b][:, j].rearrange("p g m -> p (g m)").bitcast(FP8X4),
+                    scales=xsc[b][:, j].rearrange("p g m -> p (g m)"),
+                    in_=xi[b][:, j].rearrange("p g n -> p (g n)"),
+                )
+            else:
+                nc.vector.quantize_mx(out=xc[b][:, j, gs].bitcast(FP8X4), scales=xsc[b][:, j, gs], in_=xi[b][:, j, gs])
+
+        units = [(c, j) for c in range(len(CHUNKS)) for j in range(PACK)]
+        bank = {}
+        hs = {}
+        z = {}
+        zi = {}
+        zc = {}
+        zs = {}
+
+        def product(k, w):
+            c, j = units[k]
+            b, t0, n = CHUNKS[c]
+            half, col = divmod(t0, BANK)
+            acc = psum.tile([P, BANK], F32, name="acc_" + w)
+            bank[k, w] = acc
+            for g in range(GS):
+                nc.tensor.matmul_mx(
+                    out=acc[:, :n],
+                    lhsT=xc[b][:, j, g].bitcast(FP8X4),
+                    lhsT_scale=xsc[b][:, j, g],
+                    rhs=codes[w, half][:, g, col : col + n].bitcast(FP8X4),
+                    rhs_scale=planes[w][4 * g : P, t0 : t0 + n],
+                    start=(g == 0),
+                    stop=(g == GS - 1),
+                )
+
+        def h_step(k):
+            c, j = units[k]
+            n = CHUNKS[c][2]
+            h = work.tile([P, BANK], F32, name="h")
+            hs[k] = h
+            nc.scalar.activation(
+                out=h[:, :n], in_=bank[k, "r"][:, :n], func=ACT.Identity, scale=gc[:, 1, j : j + 1], bias=gc[:, 0, j : j + 1]
+            )
+
+        us = {}
+
+        def qh_step(k):
+            n = CHUNKS[units[k][0]][2]
+            u = work.tile([P, BANK], F32, name="u")
+            us[k] = u
+            nc.vector.tensor_tensor(out=u[:, :n], in0=bank[k, "q"][:, :n], in1=hs[k][:, :n], op=ALU.mult)
+
+        def z_step(k):
+            c, j = units[k]
+            n = CHUNKS[c][2]
+            if j == 0:
+                z[c] = work.tile([P, PACK, BANK], BF16, name="z")
+            nc.vector.scalar_tensor_tensor(
+                out=z[c][:, j, :n], in0=us[k][:, :n], scalar=gf[:, j : j + 1], in1=bank[k, "p"][:, :n], op0=ALU.add, op1=ALU.mult
+            )
+
+        def interleave_z(c, lo, hi, on_scalar):
+            if c not in zi:
+                zi[c] = work.tile([P, BANK, PACK], BF16, name="zi", align_bytes=64)
+            copy(on_scalar, zi[c][:, lo:hi, :], z[c][:, :, lo:hi].rearrange("p j t -> p t j"))
+
+        def quantize_z(c, lo, hi):
+            if c not in zc:
+                zc[c] = work.tile([P, BANK], U32, name="zc", align_bytes=64)
+                zs[c] = work.tile([P, BANK], U8, name="zs", align_bytes=64)
+            nc.vector.quantize_mx(
+                out=zc[c][:, lo:hi].bitcast(FP8X4), scales=zs[c][:, lo:hi], in_=zi[c][:, lo:hi, :].rearrange("p t j -> p (t j)")
+            )
+
+        def project(c, i, on_scalar=True):
+            b, t0, n = CHUNKS[c]
+            cols = slice(i * P, (i + 1) * P)
+            acc = psum.tile([P, BANK], F32, name="acc_o")
+            nc.tensor.matmul_mx(
+                out=acc[:],
+                lhsT=zc[c][:, cols].bitcast(FP8X4),
+                lhsT_scale=zs[c][:, cols],
+                rhs=wo_codes[:].bitcast(FP8X4),
+                rhs_scale=wo_planes[:],
+                start=True,
+                stop=True,
+            )
+            res = work.tile([P, E], F32, name="res", bufs=6)
+            copy(on_scalar, res[:], acc[:])
+            nc.sync.dma_start(out=out[b, t0 + i * P : t0 + (i + 1) * P, :], in_=res[:])
+
+        def project_split(c, i):
+            b, t0, n = CHUNKS[c]
+            cols = slice(i * P, (i + 1) * P)
+            for half in range(2):
+                e = slice(half * E // 2, (half + 1) * E // 2)
+                acc = psum.tile([P, BANK], F32, name="acc_o")
+                nc.tensor.matmul_mx(
+                    out=acc[:, : E // 2],
+                    lhsT=zc[c][:, cols].bitcast(FP8X4),
+                    lhsT_scale=zs[c][:, cols],
+                    rhs=wo_codes[:, e].bitcast(FP8X4),
+                    rhs_scale=wo_planes[:, e],
+                    start=True,
+                    stop=True,
+                )
+                res = work.tile([P, E], F32, name="res", bufs=6)
+                copy(half == 1, res[:, : E // 2], acc[:, : E // 2])
+                nc.sync.dma_start(out=out[b, t0 + i * P : t0 + (i + 1) * P, e], in_=res[:, : E // 2])
+
+        nc.scalar.activation(out=warm[:, 4:5], in_=warm[:, 0:1], func=ACT.Identity)
+        for g in range(GS):
+            for t in range(PACK):
+                widen(0, g, t, t >= 3 - g)
+        interleave_x(0, 0, False, 0)
+        interleave_x(0, 0, True, 1)
+        quantize_x(0, 0, 0)
+        interleave_x(0, 1, False, 0)
+        quantize_x(0, 0, 1)
+        interleave_x(0, 1, False, 1)
+        product(0, "r")
+        interleave_x(0, 3, True)
+        quantize_x(0, 1, 0)
+        interleave_x(0, 2, False, 0)
+        quantize_x(0, 1, 1)
+        product(1, "r")
+        interleave_x(0, 2, False, 1)
+        quantize_x(0, 2)
+        nc.gpsimd.tensor_tensor(out=gc[:, 0, :], in0=coefs[:, 0, :], in1=gains[:], op=ALU.mult)
+        nc.gpsimd.tensor_tensor(out=gc[:, 1, :], in0=coefs[:, 1, :], in1=gains[:], op=ALU.mult)
+        nc.gpsimd.tensor_copy(out=gf[:], in_=gains[:])
+        quantize_x(0, 3)
+        h_step(0)
+        h_step(1)
+
+        between = {
+            3: [lambda: interleave_x(1, 0, False)],
+            4: [lambda: quantize_x(1, 0)],
+            5: [lambda: quantize_x(1, 1)],
+            6: [lambda: quantize_z(0, 0, 512), lambda: quantize_x(1, 2)],
+            7: [lambda: quantize_x(1, 3)],
+            10: [lambda: quantize_z(1, 0, 512)],
+            14: [lambda: quantize_z(2, 0, 512)],
+            18: [lambda: quantize_z(3, 0, 256)],
+            21: [lambda: interleave_z(4, 0, 128, False)],
+            22: [lambda: quantize_z(4, 0, 128)],
+        }
+        after = {
+            1: [lambda: widen(1, 0, 0, False), lambda: widen(1, 0, 1, False)],
+            2: [lambda: widen(1, 1, 0, False), lambda: widen(1, 1, 1, False)],
+        }
+        on_scalar = {
+            1: [lambda: widen(1, 0, 2, True), lambda: widen(1, 0, 3, True)],
+            2: [lambda: widen(1, 1, 2, True), lambda: widen(1, 1, 3, True)],
+            3: [lambda: interleave_x(1, 1, True), lambda: interleave_x(1, 2, "G")],
+            4: [lambda: interleave_z(0, 0, 256, "G"), lambda: interleave_z(0, 256, 512, "G")],
+            5: [lambda: interleave_x(1, 3, True)],
+            8: [lambda: interleave_z(1, 0, 256, "G"), lambda: interleave_z(1, 256, 512, "G")],
+            12: [lambda: interleave_z(2, 0, 256, "G"), lambda: interleave_z(2, 256, 512, "G")],
+            16: [lambda: interleave_z(3, 0, 256, "G")],
+        }
+        outs = {}
+        for c, first in ((0, 7), (1, 11), (2, 15), (3, 20), (4, 23)):
+            for i in range(CHUNKS[c][2] // P):
+                outs.setdefault(min(first + i, len(units) - 1), []).append((c, i))
+
+        for k in range(len(units)):
+            product(k, "q")
+            product(k, "p")
+            qh_step(k)
+            for step in on_scalar.get(k, []) if k in (4, 8, 12, 16) else []:
+                step()
+            for step in between.get(k, []):
+                step()
+            z_step(k)
+            for step in after.get(k, []):
+                step()
+            if k + 2 < len(units):
+                product(k + 2, "r")
+                h_step(k + 2)
+            for c, i in outs.get(k, []):
+                project(c, i)
+            for step in [] if k in (4, 8, 12, 16) else on_scalar.get(k, []):
+                step()
+        interleave_z(5, 0, 128, False)
+        quantize_z(5, 0, 128)
+        project_split(5, 0)

@@ -22,6 +22,7 @@ BANK = 512
 
 FLOPS = 2 * B * R * S * D * 3 + 2 * B * R * D * E + 6 * B * R * D
 
+WARM = 9
 CHUNKS = [(0, 0, 512), (0, 512, 512), (1, 0, 512), (1, 512, 256), (1, 768, 128), (1, 896, 128)]
 
 
@@ -49,14 +50,17 @@ def tile_volterrathirdordermixer_w8_kernel(
         gains = keep.tile([P, PACK], BF16, name="gains")
         gc = keep.tile([P, 2, PACK], F32, name="gc")
         gf = keep.tile([P, PACK], F32, name="gf")
+        zeros = keep.tile([P, BANK], BF16, name="zeros", align_bytes=64)
         warm = keep.tile([P, 8], F32, name="warm")
 
         scales_in = {"r": mr_scales, "q": mq_scales, "p": mp_scales}
         words_in = {"r": mr_words, "q": mq_words, "p": mp_words}
 
+        nc.gpsimd.memset(warm[:], 0.0)
+        nc.scalar.dma_start(out=xs[:], in_=x_scale[0].rearrange("(g p t) o -> p g (t o)", g=GS, t=PACK))
         nc.gpsimd.dma_start(out=coefs[:], in_=coef.rearrange("c (p j) -> p c j", j=PACK))
         nc.gpsimd.dma_start(out=gains[:], in_=gain.rearrange("(p j) -> p j", j=PACK))
-        nc.gpsimd.memset(warm[:], 0.0)
+        nc.vector.memset(zeros[:], 0.0)
         for w in "rqp":
             nc.vector.memset(planes[w][:].bitcast(I32), 0)
         nc.vector.memset(wo_planes[:].bitcast(I32), 0)
@@ -77,14 +81,14 @@ def tile_volterrathirdordermixer_w8_kernel(
                 out=codes[w, h][:].bitcast(I32), in_=view[:, :, h * BANK * PACK : (h + 1) * BANK * PACK].bitcast(I32)
             )
 
-        nc.sync.dma_start(out=xs[:], in_=x_scale[0].rearrange("(g p t) o -> p g (t o)", g=GS, t=PACK))
         load_x(0, 0)
         load_x(0, 1)
         load_scales("r")
         load_codes("r", 0)
-        for w in "qp":
-            load_codes(w, 0)
-            load_scales(w)
+        load_codes("q", 0)
+        load_scales("q")
+        load_codes("p", 0)
+        load_scales("p")
         load_x(1, 0)
         load_x(1, 1)
         for w in "rqp":
@@ -229,6 +233,9 @@ def tile_volterrathirdordermixer_w8_kernel(
                 copy(half == 1, res[:, : E // 2], acc[:, : E // 2])
                 nc.sync.dma_start(out=out[b, t0 + i * P : t0 + (i + 1) * P, e], in_=res[:, : E // 2])
 
+        idle = psum.tile([P, BANK], F32, name="acc_o")
+        for i in range(WARM):
+            nc.tensor.matmul(out=idle[:], lhsT=zeros[:, :P], rhs=zeros[:], start=True, stop=True)
         nc.scalar.activation(out=warm[:, 4:5], in_=warm[:, 0:1], func=ACT.Identity)
         for g in range(GS):
             for t in range(PACK):
@@ -255,11 +262,10 @@ def tile_volterrathirdordermixer_w8_kernel(
         h_step(1)
 
         between = {
-            3: [lambda: interleave_x(1, 0, False)],
-            4: [lambda: quantize_x(1, 0)],
-            5: [lambda: quantize_x(1, 1)],
-            6: [lambda: quantize_z(0, 0, 512), lambda: quantize_x(1, 2)],
-            7: [lambda: quantize_x(1, 3)],
+            4: [lambda: interleave_x(1, 0, False)],
+            5: [lambda: quantize_x(1, 0), lambda: quantize_x(1, 1)],
+            6: [lambda: quantize_z(0, 0, 512)],
+            7: [lambda: quantize_x(1, 2), lambda: quantize_x(1, 3)],
             10: [lambda: quantize_z(1, 0, 512)],
             14: [lambda: quantize_z(2, 0, 512)],
             18: [lambda: quantize_z(3, 0, 256)],
@@ -267,14 +273,14 @@ def tile_volterrathirdordermixer_w8_kernel(
             22: [lambda: quantize_z(4, 0, 128)],
         }
         after = {
-            1: [lambda: widen(1, 0, 0, False), lambda: widen(1, 0, 1, False)],
-            2: [lambda: widen(1, 1, 0, False), lambda: widen(1, 1, 1, False)],
+            2: [lambda: widen(1, 0, 0, False), lambda: widen(1, 0, 1, False)],
+            3: [lambda: widen(1, 1, 0, False), lambda: widen(1, 1, 1, False)],
         }
         on_scalar = {
-            1: [lambda: widen(1, 0, 2, True), lambda: widen(1, 0, 3, True)],
-            2: [lambda: widen(1, 1, 2, True), lambda: widen(1, 1, 3, True)],
-            3: [lambda: interleave_x(1, 1, True), lambda: interleave_x(1, 2, "G")],
-            4: [lambda: interleave_z(0, 0, 256, "G"), lambda: interleave_z(0, 256, 512, "G")],
+            1: [lambda: widen(1, 0, 2, True)],
+            2: [lambda: widen(1, 0, 3, True), lambda: widen(1, 1, 2, True)],
+            3: [lambda: widen(1, 1, 3, True), lambda: interleave_x(1, 1, True)],
+            4: [lambda: interleave_z(0, 0, 256, "G"), lambda: interleave_z(0, 256, 512, "G"), lambda: interleave_x(1, 2, "G")],
             5: [lambda: interleave_x(1, 3, True)],
             8: [lambda: interleave_z(1, 0, 256, "G"), lambda: interleave_z(1, 256, 512, "G")],
             12: [lambda: interleave_z(2, 0, 256, "G"), lambda: interleave_z(2, 256, 512, "G")],

@@ -23,6 +23,13 @@ BANK = 512
 FLOPS = 2 * B * R * S * D * 3 + 2 * B * R * D * E + 6 * B * R * D
 
 WARM = 9
+PLAN = {
+    'Va': {1: [('W', 1, 1, 3), ('W', 1, 0, 1)], 2: [('W', 1, 0, 2)], 3: [('W', 1, 1, 1)], 4: [('I', 1, 0)], 5: [('Q', 1, 0)], 6: [('Q', 1, 3)], 7: [('Q', 1, 2)], 8: [('IZ', 0, 0, 256)], 9: [('QZ', 0, 0, 256)], 10: [('QZ', 1, 0, 256)], 12: [('IZ', 2, 0, 256)], 14: [('QZ', 1, 256, 512)], 15: [('QZ', 2, 0, 256)], 16: [('QZ', 2, 256, 512)], 17: [('IZ', 3, 0, 256)], 19: [('QZ', 3, 0, 256)], 20: [('IZ', 4, 0, 128)], 22: [('QZ', 4, 0, 128)]},
+    'Vb': {5: [('Q', 1, 1)], 10: [('QZ', 0, 256, 512)]},
+    'Sa': {0: [('W', 1, 1, 2)], 4: [('I', 1, 3)], 6: [('IZ', 0, 256, 512)], 10: [('IZ', 1, 256, 512)]},
+    'Sb': {1: [('W', 1, 0, 3), ('W', 1, 0, 0), ('W', 1, 1, 0)], 4: [('I', 1, 1)], 5: [('I', 1, 2)], 7: [('IZ', 1, 0, 256)], 12: [('IZ', 2, 256, 512)]},
+    'O': {10: [(0, 0, 'S'), (0, 1, 'S')], 11: [(0, 3, 'S'), (0, 2, 'S')], 13: [(1, 1, 'S')], 14: [(1, 0, 'S')], 16: [(2, 1, 'S'), (1, 2, 'S')], 17: [(1, 3, 'S')], 18: [(2, 0, 'S')], 19: [(2, 3, 'S')], 20: [(2, 2, 'S')], 22: [(3, 1, 'S')], 23: [(4, 0, 'S'), (3, 0, 'S')]},
+}
 CHUNKS = [(0, 0, 512), (0, 512, 512), (1, 0, 512), (1, 512, 256), (1, 768, 128), (1, 896, 128)]
 
 
@@ -258,57 +265,43 @@ def tile_volterrathirdordermixer_w8_kernel(
         nc.gpsimd.tensor_tensor(out=gc[:, 1, :], in0=coefs[:, 1, :], in1=gains[:], op=ALU.mult)
         nc.gpsimd.tensor_copy(out=gf[:], in_=gains[:])
         quantize_x(0, 3)
+        product(0, "q")
         h_step(0)
         h_step(1)
 
-        between = {
-            4: [lambda: interleave_x(1, 0, False)],
-            5: [lambda: quantize_x(1, 0), lambda: quantize_x(1, 1)],
-            6: [lambda: quantize_z(0, 0, 512)],
-            7: [lambda: quantize_x(1, 2), lambda: quantize_x(1, 3)],
-            10: [lambda: quantize_z(1, 0, 512)],
-            14: [lambda: quantize_z(2, 0, 512)],
-            18: [lambda: quantize_z(3, 0, 256)],
-            21: [lambda: interleave_z(4, 0, 128, False)],
-            22: [lambda: quantize_z(4, 0, 128)],
-        }
-        after = {
-            2: [lambda: widen(1, 0, 0, False), lambda: widen(1, 0, 1, False)],
-            3: [lambda: widen(1, 1, 0, False), lambda: widen(1, 1, 1, False)],
-        }
-        on_scalar = {
-            1: [lambda: widen(1, 0, 2, True)],
-            2: [lambda: widen(1, 0, 3, True), lambda: widen(1, 1, 2, True)],
-            3: [lambda: widen(1, 1, 3, True), lambda: interleave_x(1, 1, True)],
-            4: [lambda: interleave_z(0, 0, 256, "G"), lambda: interleave_z(0, 256, 512, "G"), lambda: interleave_x(1, 2, "G")],
-            5: [lambda: interleave_x(1, 3, True)],
-            8: [lambda: interleave_z(1, 0, 256, "G"), lambda: interleave_z(1, 256, 512, "G")],
-            12: [lambda: interleave_z(2, 0, 256, "G"), lambda: interleave_z(2, 256, 512, "G")],
-            16: [lambda: interleave_z(3, 0, 256, "G")],
-        }
-        outs = {}
-        for c, first in ((0, 7), (1, 11), (2, 15), (3, 20), (4, 23)):
-            for i in range(CHUNKS[c][2] // P):
-                outs.setdefault(min(first + i, len(units) - 1), []).append((c, i))
+        def do(step, on_scalar):
+            kind = step[0]
+            if kind == "W":
+                widen(*step[1:], on_scalar)
+            elif kind == "I":
+                interleave_x(*step[1:], on_scalar)
+            elif kind == "Q":
+                quantize_x(*step[1:])
+            elif kind == "IZ":
+                interleave_z(*step[1:], on_scalar)
+            elif kind == "QZ":
+                quantize_z(*step[1:])
 
         for k in range(len(units)):
-            product(k, "q")
-            product(k, "p")
-            qh_step(k)
-            for step in on_scalar.get(k, []) if k in (4, 8, 12, 16) else []:
-                step()
-            for step in between.get(k, []):
-                step()
-            z_step(k)
-            for step in after.get(k, []):
-                step()
+            if k + 1 < len(units):
+                product(k + 1, "q")
             if k + 2 < len(units):
                 product(k + 2, "r")
+            product(k, "p")
+            qh_step(k)
+            for s in PLAN["Va"].get(k, []):
+                do(s, False)
+            z_step(k)
+            for s in PLAN["Vb"].get(k, []):
+                do(s, False)
+            for s in PLAN["Sa"].get(k, []):
+                do(s, True)
+            if k + 2 < len(units):
                 h_step(k + 2)
-            for c, i in outs.get(k, []):
-                project(c, i)
-            for step in [] if k in (4, 8, 12, 16) else on_scalar.get(k, []):
-                step()
+            for c, i, eng in PLAN["O"].get(k, []):
+                project(c, i, eng == "S")
+            for s in PLAN["Sb"].get(k, []):
+                do(s, True)
         interleave_z(5, 0, 128, False)
         quantize_z(5, 0, 128)
         project_split(5, 0)

@@ -17,76 +17,142 @@ B, S, R, D, E = 2, 1024, 1024, 512, 512
 P = 128
 PACK = 4
 K_PASS = P * PACK
-GS = S // K_PASS
+GROUPS = S // K_PASS
 BANK = 512
+RUN = 4
 
-FLOPS = 2 * B * R * S * D * 3 + 2 * B * R * D * E + 6 * B * R * D
+FLOPS = 3 * 2 * B * R * S * D + 2 * B * R * D * E + 6 * B * R * D
 
-WARM = 9
-PLAN = {
-    'Va': {1: [('W', 1, 1, 3), ('W', 1, 0, 1)], 2: [('W', 1, 0, 2)], 3: [('W', 1, 1, 1)], 4: [('I', 1, 0)], 5: [('Q', 1, 0)], 6: [('Q', 1, 3)], 7: [('Q', 1, 2)], 8: [('IZ', 0, 0, 256)], 9: [('QZ', 0, 0, 256)], 10: [('QZ', 1, 0, 256)], 12: [('IZ', 2, 0, 256)], 14: [('QZ', 1, 256, 512)], 15: [('QZ', 2, 0, 256)], 16: [('QZ', 2, 256, 512)], 17: [('IZ', 3, 0, 256)], 19: [('QZ', 3, 0, 256)], 20: [('IZ', 4, 0, 128)], 22: [('QZ', 4, 0, 128)]},
-    'Vb': {5: [('Q', 1, 1)], 10: [('QZ', 0, 256, 512)]},
-    'Sa': {0: [('W', 1, 1, 2)], 4: [('I', 1, 3)], 6: [('IZ', 0, 256, 512)], 10: [('IZ', 1, 256, 512)]},
-    'Sb': {1: [('W', 1, 0, 3), ('W', 1, 0, 0), ('W', 1, 1, 0)], 4: [('I', 1, 1)], 5: [('I', 1, 2)], 7: [('IZ', 1, 0, 256)], 12: [('IZ', 2, 256, 512)]},
-    'O': {10: [(0, 0, 'S'), (0, 1, 'S')], 11: [(0, 3, 'S'), (0, 2, 'S')], 13: [(1, 1, 'S')], 14: [(1, 0, 'S')], 16: [(2, 1, 'S'), (1, 2, 'S')], 17: [(1, 3, 'S')], 18: [(2, 0, 'S')], 19: [(2, 3, 'S')], 20: [(2, 2, 'S')], 22: [(3, 1, 'S')], 23: [(4, 0, 'S'), (3, 0, 'S')]},
-}
 CHUNKS = [(0, 0, 512), (0, 512, 512), (1, 0, 512), (1, 512, 256), (1, 768, 128), (1, 896, 128)]
+UNITS = [(c, j) for c in range(len(CHUNKS)) for j in range(PACK)]
+
+PLANE_START = {"r": 0, "q": 4, "p": 8, "o": 12}
+
+WARM_UP = 9
+
+VECTOR_BEFORE_Z = {
+    2: [("widen", 1, 1, 1)],
+    3: [("interleave_x", 1, 0)],
+    4: [("quantize_x", 1, 0), ("quantize_x", 1, 1)],
+    9: [("quantize_z", 1, 0, 256)],
+    11: [("quantize_z", 1, 256, 512)],
+    12: [("interleave_z", 2, 0, 256)],
+    13: [("quantize_z", 2, 0, 256)],
+}
+VECTOR_BEHIND_Z = {
+    0: [("widen", 1, 0, 3)],
+    3: [("interleave_x", 1, 1)],
+    6: [("quantize_x", 1, 2)],
+    7: [("quantize_x", 1, 3), ("quantize_z", 0, 256, 512)],
+    8: [("quantize_z", 0, 0, 256)],
+    14: [("quantize_z", 2, 256, 512)],
+    16: [("interleave_z", 3, 0, 256)],
+    19: [("quantize_z", 3, 0, 256), ("interleave_z", 4, 0, 128)],
+    20: [("quantize_z", 4, 0, 128)],
+}
+SCALAR_BEFORE_H = {
+    0: [("widen", 1, 0, 2), ("widen", 1, 0, 1)],
+    1: [("widen", 1, 0, 0)],
+    3: [("interleave_x", 1, 3)],
+    4: [("interleave_z", 0, 0, 256)],
+    10: [("interleave_z", 1, 256, 512)],
+    12: [("interleave_z", 2, 256, 512)],
+}
+SCALAR_BEHIND_H = {
+    1: [("widen", 1, 1, 2)],
+    2: [("widen", 1, 1, 3), ("widen", 1, 1, 0)],
+    5: [("interleave_x", 1, 2)],
+    6: [("interleave_z", 0, 256, 512)],
+    7: [("interleave_z", 1, 0, 256)],
+}
+PROJECTIONS = {
+    10: [(0, 2, "scalar"), (1, 0, "scalar")],
+    11: [(0, 1, "scalar")],
+    12: [(0, 3, "scalar"), (0, 0, "vector")],
+    14: [(2, 0, "scalar"), (1, 2, "scalar")],
+    15: [(1, 3, "scalar")],
+    17: [(2, 1, "scalar")],
+    18: [(1, 1, "scalar")],
+    19: [(2, 2, "scalar")],
+    20: [(3, 0, "scalar")],
+    21: [(3, 1, "scalar")],
+    23: [(4, 0, "scalar"), (2, 3, "scalar")],
+}
 
 
 def tile_volterrathirdordermixer_w8_kernel(
-    tc, x_bytes, x_scale, mp_words, mp_scales, mq_words, mq_scales, mr_words, mr_scales, coef, gain, wo_words, wo_scales, out
+    tc,
+    x_bytes,
+    x_scale,
+    mp_words,
+    mp_scales,
+    mq_words,
+    mq_scales,
+    mr_words,
+    mr_scales,
+    coef,
+    gain,
+    wo_words,
+    wo_scales,
+    out,
 ):
     nc = tc.nc
+    words_in = {"r": mr_words, "q": mq_words, "p": mp_words}
+    scales_in = {"r": mr_scales, "q": mq_scales, "p": mp_scales}
+
     with ExitStack() as ctx:
         keep = ctx.enter_context(tc.tile_pool(name="keep", bufs=1))
         work = ctx.enter_context(tc.tile_pool(name="work", bufs=3))
         psum = ctx.enter_context(tc.psum_pool(name="psum", bufs=2))
         ctx.enter_context(tc.manual_schedule())
 
-        xb = [[keep.tile([P, PACK * D], U8, name="xb%d%d" % (b, g)) for g in range(GS)] for b in range(B)]
-        xs = keep.tile([P, GS, PACK], F32, name="xs")
-        xw = [keep.tile([P, GS, PACK, D], BF16, name="xw%d" % b) for b in range(B)]
-        xi = [keep.tile([P, PACK, GS, P * PACK], BF16, name="xi%d" % b, align_bytes=64) for b in range(B)]
-        xc = [keep.tile([P, PACK, GS, P], U32, name="xc%d" % b, align_bytes=64) for b in range(B)]
-        xsc = [keep.tile([P, PACK, GS, P], U8, name="xsc%d" % b, align_bytes=64) for b in range(B)]
-        planes = {w: keep.tile([P, R], U8, name="planes_" + w, align_bytes=64) for w in "rqp"}
-        codes = {(w, h): keep.tile([P, GS, BANK], U32, name="codes_%s%d" % (w, h), align_bytes=64) for w in "rqp" for h in range(2)}
-        wo_planes = keep.tile([P, E], U8, name="wo_planes", align_bytes=64)
+        x_raw = [[keep.tile([P, PACK * D], U8, name="x_raw%d%d" % (b, g)) for g in range(GROUPS)] for b in range(B)]
+        x_factor = keep.tile([P, GROUPS, PACK], F32, name="x_factor")
+        x_wide = [keep.tile([P, GROUPS, PACK, D], BF16, name="x_wide%d" % b) for b in range(B)]
+        x_mixed = [keep.tile([P, PACK, GROUPS, P * PACK], BF16, name="x_mixed%d" % b, align_bytes=64) for b in range(B)]
+        x_codes = [keep.tile([P, PACK, GROUPS, P], U32, name="x_codes%d" % b, align_bytes=64) for b in range(B)]
+        x_planes = [keep.tile([P, PACK, GROUPS, P], U8, name="x_planes%d" % b, align_bytes=64) for b in range(B)]
+
+        m_codes = {
+            (w, half): keep.tile([P, GROUPS, BANK], U32, name="m_codes_%s%d" % (w, half), align_bytes=64)
+            for w in "rqp"
+            for half in range(R // BANK)
+        }
+        m_planes = {w: keep.tile([P, GROUPS, R], U8, name="m_planes_" + w, align_bytes=64) for w in "rqp"}
         wo_codes = keep.tile([P, E], U32, name="wo_codes", align_bytes=64)
+        wo_planes = keep.tile([P, E], U8, name="wo_planes", align_bytes=64)
+
         coefs = keep.tile([P, 2, PACK], BF16, name="coefs")
         gains = keep.tile([P, PACK], BF16, name="gains")
-        gc = keep.tile([P, 2, PACK], F32, name="gc")
-        gf = keep.tile([P, PACK], F32, name="gf")
+        gain_coef = keep.tile([P, 2, PACK], F32, name="gain_coef")
         zeros = keep.tile([P, BANK], BF16, name="zeros", align_bytes=64)
-        warm = keep.tile([P, 8], F32, name="warm")
+        first_act = keep.tile([P, 8], F32, name="first_act")
 
-        scales_in = {"r": mr_scales, "q": mq_scales, "p": mp_scales}
-        words_in = {"r": mr_words, "q": mq_words, "p": mp_words}
+        def zero_plane(plane):
+            nc.vector.memset(plane.bitcast(I32), 0)
 
-        nc.gpsimd.memset(warm[:], 0.0)
-        nc.scalar.dma_start(out=xs[:], in_=x_scale[0].rearrange("(g p t) o -> p g (t o)", g=GS, t=PACK))
+        def load_x(b, g):
+            rows = x_bytes[b, g * K_PASS : (g + 1) * K_PASS, :]
+            nc.sync.dma_start(out=x_raw[b][g][:], in_=rows.rearrange("(p t) d -> p (t d)", t=PACK))
+
+        def load_codes(w, half):
+            view = words_in[w].rearrange("g p n t -> p g (n t)")
+            cols = slice(half * BANK * PACK, (half + 1) * BANK * PACK)
+            nc.sync.dma_start(out=m_codes[w, half][:].bitcast(I32), in_=view[:, :, cols].bitcast(I32))
+
+        def load_scales(w):
+            view = scales_in[w].rearrange("g (q i) n -> i q g n", i=4)
+            for i in range(4):
+                nc.sync.dma_start(out=m_planes[w][PLANE_START[w] + i : P : 32, :, :].bitcast(I32), in_=view[i].bitcast(I32))
+
+        nc.gpsimd.memset(first_act[:], 0.0)
+        nc.scalar.dma_start(out=x_factor[:], in_=x_scale[0].rearrange("(g p t) o -> p g (t o)", g=GROUPS, t=PACK))
         nc.gpsimd.dma_start(out=coefs[:], in_=coef.rearrange("c (p j) -> p c j", j=PACK))
         nc.gpsimd.dma_start(out=gains[:], in_=gain.rearrange("(p j) -> p j", j=PACK))
         nc.vector.memset(zeros[:], 0.0)
         for w in "rqp":
-            nc.vector.memset(planes[w][:].bitcast(I32), 0)
-        nc.vector.memset(wo_planes[:].bitcast(I32), 0)
-
-        def load_x(b, g):
-            nc.sync.dma_start(out=xb[b][g][:], in_=x_bytes[b, g * K_PASS : (g + 1) * K_PASS, :].rearrange("(p t) d -> p (t d)", t=PACK))
-
-        def load_scales(w):
-            for quad in range(4):
-                nc.sync.dma_start(
-                    out=planes[w][32 * quad : 32 * quad + 8, :].bitcast(I32),
-                    in_=scales_in[w][:, 4 * quad : 4 * quad + 4, :].bitcast(I32),
-                )
-
-        def load_codes(w, h):
-            view = words_in[w].rearrange("g p n t -> p g (n t)")
-            nc.sync.dma_start(
-                out=codes[w, h][:].bitcast(I32), in_=view[:, :, h * BANK * PACK : (h + 1) * BANK * PACK].bitcast(I32)
-            )
+            zero_plane(m_planes[w][:].rearrange("p g n -> p (g n)"))
+        zero_plane(wo_planes[:])
 
         load_x(0, 0)
         load_x(0, 1)
@@ -100,208 +166,194 @@ def tile_volterrathirdordermixer_w8_kernel(
         load_x(1, 1)
         for w in "rqp":
             load_codes(w, 1)
-        for quad in range(4):
-            nc.sync.dma_start(
-                out=wo_planes[32 * quad : 32 * quad + 4, :].bitcast(I32), in_=wo_scales[0, 4 * quad : 4 * quad + 4, :].bitcast(I32)
-            )
+        wo_view = wo_scales[0].rearrange("(q i) n -> i q n", i=4)
+        for i in range(4):
+            nc.sync.dma_start(out=wo_planes[PLANE_START["o"] + i : P : 32, :].bitcast(I32), in_=wo_view[i].bitcast(I32))
         nc.sync.dma_start(out=wo_codes[:].bitcast(I32), in_=wo_words[0].rearrange("p n t -> p (n t)").bitcast(I32))
 
-        def widen(b, g, t, on_scalar):
-            src = xb[b][g][:, t * D : (t + 1) * D].bitcast(FP8)
-            if on_scalar:
-                nc.scalar.activation(out=xw[b][:, g, t, :], in_=src, func=ACT.Copy, scale=xs[:, g, t : t + 1])
-            else:
-                nc.vector.tensor_scalar(out=xw[b][:, g, t, :], in0=src, scalar1=xs[:, g, t : t + 1], scalar2=None, op0=ALU.mult)
-
-        def copy(on_scalar, dst, src):
-            if on_scalar == "G":
-                nc.gpsimd.tensor_scalar(out=dst, in0=src, scalar1=1.0, scalar2=0.0, op0=ALU.mult, op1=ALU.add)
-            elif on_scalar:
+        def copy(engine, dst, src):
+            if engine == "scalar":
                 nc.scalar.copy(out=dst, in_=src)
             else:
                 nc.vector.tensor_copy(out=dst, in_=src)
 
-        def interleave_x(b, j, on_scalar, gs=None):
-            if gs is None:
-                src = xw[b][:].rearrange("p g t (m j) -> p j g m t", j=PACK)[:, j]
-                dst = xi[b][:, j].rearrange("p g (m t) -> p g m t", t=PACK)
+        def widen(engine, b, g, t):
+            src = x_raw[b][g][:, t * D : (t + 1) * D].bitcast(FP8)
+            dst = x_wide[b][:, g, t, :]
+            factor = x_factor[:, g, t : t + 1]
+            if engine == "scalar":
+                nc.scalar.activation(out=dst, in_=src, func=ACT.Copy, scale=factor)
             else:
-                src = xw[b][:, gs].rearrange("p t (m j) -> p j m t", j=PACK)[:, j]
-                dst = xi[b][:, j, gs].rearrange("p (m t) -> p m t", t=PACK)
-            copy(on_scalar, dst, src)
+                nc.vector.tensor_scalar(out=dst, in0=src, scalar1=factor, scalar2=None, op0=ALU.mult)
 
-        def quantize_x(b, j, gs=None):
-            if gs is None:
-                nc.vector.quantize_mx(
-                    out=xc[b][:, j].rearrange("p g m -> p (g m)").bitcast(FP8X4),
-                    scales=xsc[b][:, j].rearrange("p g m -> p (g m)"),
-                    in_=xi[b][:, j].rearrange("p g n -> p (g n)"),
-                )
-            else:
-                nc.vector.quantize_mx(out=xc[b][:, j, gs].bitcast(FP8X4), scales=xsc[b][:, j, gs], in_=xi[b][:, j, gs])
+        def interleave_group(engine, b, j, g):
+            src = x_wide[b][:, g].rearrange("p t (c i j) -> p j c t i", i=RUN, j=PACK)[:, j]
+            dst = x_mixed[b][:, j, g].rearrange("p (c i t) -> p c t i", i=RUN, t=PACK)
+            copy(engine, dst, src)
 
-        units = [(c, j) for c in range(len(CHUNKS)) for j in range(PACK)]
-        bank = {}
-        hs = {}
-        z = {}
-        zi = {}
-        zc = {}
-        zs = {}
+        def interleave_x(engine, b, j):
+            for g in range(GROUPS):
+                interleave_group(engine, b, j, g)
+
+        def quantize_group(b, j, g):
+            nc.vector.quantize_mx(out=x_codes[b][:, j, g].bitcast(FP8X4), scales=x_planes[b][:, j, g], in_=x_mixed[b][:, j, g])
+
+        def quantize_x(engine, b, j):
+            nc.vector.quantize_mx(
+                out=x_codes[b][:, j].rearrange("p g m -> p (g m)").bitcast(FP8X4),
+                scales=x_planes[b][:, j].rearrange("p g m -> p (g m)"),
+                in_=x_mixed[b][:, j].rearrange("p g n -> p (g n)"),
+            )
+
+        banks, h_tiles, u_tiles = {}, {}, {}
+        z_wide, z_mixed, z_codes, z_planes = {}, {}, {}, {}
 
         def product(k, w):
-            c, j = units[k]
+            c, j = UNITS[k]
             b, t0, n = CHUNKS[c]
             half, col = divmod(t0, BANK)
-            acc = psum.tile([P, BANK], F32, name="acc_" + w)
-            bank[k, w] = acc
-            for g in range(GS):
+            bank = psum.tile([P, BANK], F32, name="bank_" + w)
+            banks[k, w] = bank
+            for g in range(GROUPS):
                 nc.tensor.matmul_mx(
-                    out=acc[:, :n],
-                    lhsT=xc[b][:, j, g].bitcast(FP8X4),
-                    lhsT_scale=xsc[b][:, j, g],
-                    rhs=codes[w, half][:, g, col : col + n].bitcast(FP8X4),
-                    rhs_scale=planes[w][4 * g : P, t0 : t0 + n],
+                    out=bank[:, :n],
+                    lhsT=x_codes[b][:, j, g].bitcast(FP8X4),
+                    lhsT_scale=x_planes[b][:, j, g],
+                    rhs=m_codes[w, half][:, g, col : col + n].bitcast(FP8X4),
+                    rhs_scale=m_planes[w][PLANE_START[w] : P, g, t0 : t0 + n],
                     start=(g == 0),
-                    stop=(g == GS - 1),
+                    stop=(g == GROUPS - 1),
                 )
 
-        def h_step(k):
-            c, j = units[k]
+        def gain_h(k):
+            c, j = UNITS[k]
             n = CHUNKS[c][2]
             h = work.tile([P, BANK], F32, name="h")
-            hs[k] = h
+            h_tiles[k] = h
             nc.scalar.activation(
-                out=h[:, :n], in_=bank[k, "r"][:, :n], func=ACT.Identity, scale=gc[:, 1, j : j + 1], bias=gc[:, 0, j : j + 1]
+                out=h[:, :n],
+                in_=banks[k, "r"][:, :n],
+                func=ACT.Identity,
+                scale=gain_coef[:, 1, j : j + 1],
+                bias=gain_coef[:, 0, j : j + 1],
             )
 
-        us = {}
-
-        def qh_step(k):
-            n = CHUNKS[units[k][0]][2]
+        def q_times_h(k):
+            n = CHUNKS[UNITS[k][0]][2]
             u = work.tile([P, BANK], F32, name="u")
-            us[k] = u
-            nc.vector.tensor_tensor(out=u[:, :n], in0=bank[k, "q"][:, :n], in1=hs[k][:, :n], op=ALU.mult)
+            u_tiles[k] = u
+            nc.vector.tensor_tensor(out=u[:, :n], in0=banks[k, "q"][:, :n], in1=h_tiles[k][:, :n], op=ALU.mult)
 
-        def z_step(k):
-            c, j = units[k]
+        def make_z(k):
+            c, j = UNITS[k]
             n = CHUNKS[c][2]
             if j == 0:
-                z[c] = work.tile([P, PACK, BANK], BF16, name="z")
+                z_wide[c] = work.tile([P, PACK, BANK], BF16, name="z_wide")
             nc.vector.scalar_tensor_tensor(
-                out=z[c][:, j, :n], in0=us[k][:, :n], scalar=gf[:, j : j + 1], in1=bank[k, "p"][:, :n], op0=ALU.add, op1=ALU.mult
+                out=z_wide[c][:, j, :n],
+                in0=u_tiles[k][:, :n],
+                scalar=gains[:, j : j + 1],
+                in1=banks[k, "p"][:, :n],
+                op0=ALU.add,
+                op1=ALU.mult,
             )
 
-        def interleave_z(c, lo, hi, on_scalar):
-            if c not in zi:
-                zi[c] = work.tile([P, BANK, PACK], BF16, name="zi", align_bytes=64)
-            copy(on_scalar, zi[c][:, lo:hi, :], z[c][:, :, lo:hi].rearrange("p j t -> p t j"))
+        def interleave_z(engine, c, lo, hi):
+            if c not in z_mixed:
+                z_mixed[c] = work.tile([P, BANK, PACK], BF16, name="z_mixed", align_bytes=64)
+            src = z_wide[c][:, :, lo:hi].rearrange("p j (c i) -> p c j i", i=RUN)
+            dst = z_mixed[c][:, lo:hi, :].rearrange("p (c i) j -> p c j i", i=RUN)
+            copy(engine, dst, src)
 
-        def quantize_z(c, lo, hi):
-            if c not in zc:
-                zc[c] = work.tile([P, BANK], U32, name="zc", align_bytes=64)
-                zs[c] = work.tile([P, BANK], U8, name="zs", align_bytes=64)
+        def quantize_z(engine, c, lo, hi):
+            if c not in z_codes:
+                z_codes[c] = work.tile([P, BANK], U32, name="z_codes", align_bytes=64)
+                z_planes[c] = work.tile([P, BANK], U8, name="z_planes", align_bytes=64)
             nc.vector.quantize_mx(
-                out=zc[c][:, lo:hi].bitcast(FP8X4), scales=zs[c][:, lo:hi], in_=zi[c][:, lo:hi, :].rearrange("p t j -> p (t j)")
+                out=z_codes[c][:, lo:hi].bitcast(FP8X4),
+                scales=z_planes[c][:, lo:hi],
+                in_=z_mixed[c][:, lo:hi, :].rearrange("p t j -> p (t j)"),
             )
 
-        def project(c, i, on_scalar=True):
+        def project(c, tile_index, engine, cols=slice(0, E)):
             b, t0, n = CHUNKS[c]
-            cols = slice(i * P, (i + 1) * P)
-            acc = psum.tile([P, BANK], F32, name="acc_o")
+            width = cols.stop - cols.start
+            times = slice(tile_index * P, (tile_index + 1) * P)
+            bank = psum.tile([P, BANK], F32, name="bank_o")
             nc.tensor.matmul_mx(
-                out=acc[:],
-                lhsT=zc[c][:, cols].bitcast(FP8X4),
-                lhsT_scale=zs[c][:, cols],
-                rhs=wo_codes[:].bitcast(FP8X4),
-                rhs_scale=wo_planes[:],
+                out=bank[:, :width],
+                lhsT=z_codes[c][:, times].bitcast(FP8X4),
+                lhsT_scale=z_planes[c][:, times],
+                rhs=wo_codes[:, cols].bitcast(FP8X4),
+                rhs_scale=wo_planes[PLANE_START["o"] : P, cols],
                 start=True,
                 stop=True,
             )
-            res = work.tile([P, E], F32, name="res", bufs=6)
-            copy(on_scalar, res[:], acc[:])
-            nc.sync.dma_start(out=out[b, t0 + i * P : t0 + (i + 1) * P, :], in_=res[:])
+            result = work.tile([P, E], F32, name="result", bufs=6)
+            copy(engine, result[:, :width], bank[:, :width])
+            nc.sync.dma_start(out=out[b, t0 + times.start : t0 + times.stop, cols], in_=result[:, :width])
 
-        def project_split(c, i):
-            b, t0, n = CHUNKS[c]
-            cols = slice(i * P, (i + 1) * P)
-            for half in range(2):
-                e = slice(half * E // 2, (half + 1) * E // 2)
-                acc = psum.tile([P, BANK], F32, name="acc_o")
-                nc.tensor.matmul_mx(
-                    out=acc[:, : E // 2],
-                    lhsT=zc[c][:, cols].bitcast(FP8X4),
-                    lhsT_scale=zs[c][:, cols],
-                    rhs=wo_codes[:, e].bitcast(FP8X4),
-                    rhs_scale=wo_planes[:, e],
-                    start=True,
-                    stop=True,
-                )
-                res = work.tile([P, E], F32, name="res", bufs=6)
-                copy(half == 1, res[:, : E // 2], acc[:, : E // 2])
-                nc.sync.dma_start(out=out[b, t0 + i * P : t0 + (i + 1) * P, e], in_=res[:, : E // 2])
-
-        idle = psum.tile([P, BANK], F32, name="acc_o")
-        for i in range(WARM):
+        idle = psum.tile([P, BANK], F32, name="bank_o")
+        for i in range(WARM_UP):
             nc.tensor.matmul(out=idle[:], lhsT=zeros[:, :P], rhs=zeros[:], start=True, stop=True)
-        nc.scalar.activation(out=warm[:, 4:5], in_=warm[:, 0:1], func=ACT.Identity)
-        for g in range(GS):
+        nc.scalar.activation(out=first_act[:, 4:5], in_=first_act[:, 0:1], func=ACT.Identity)
+        for g in range(GROUPS):
             for t in range(PACK):
-                widen(0, g, t, t >= 3 - g)
-        interleave_x(0, 0, False, 0)
-        interleave_x(0, 0, True, 1)
-        quantize_x(0, 0, 0)
-        interleave_x(0, 1, False, 0)
-        quantize_x(0, 0, 1)
-        interleave_x(0, 1, False, 1)
+                widen("vector" if t < 3 - g else "scalar", 0, g, t)
+        interleave_group("vector", 0, 0, 0)
+        interleave_group("scalar", 0, 0, 1)
+        quantize_group(0, 0, 0)
+        interleave_group("vector", 0, 1, 0)
+        quantize_group(0, 0, 1)
+        interleave_group("vector", 0, 1, 1)
         product(0, "r")
-        interleave_x(0, 3, True)
-        quantize_x(0, 1, 0)
-        interleave_x(0, 2, False, 0)
-        quantize_x(0, 1, 1)
+        interleave_x("scalar", 0, 3)
+        quantize_group(0, 1, 0)
+        interleave_group("vector", 0, 2, 0)
+        quantize_group(0, 1, 1)
         product(1, "r")
-        interleave_x(0, 2, False, 1)
-        quantize_x(0, 2)
-        nc.gpsimd.tensor_tensor(out=gc[:, 0, :], in0=coefs[:, 0, :], in1=gains[:], op=ALU.mult)
-        nc.gpsimd.tensor_tensor(out=gc[:, 1, :], in0=coefs[:, 1, :], in1=gains[:], op=ALU.mult)
-        nc.gpsimd.tensor_copy(out=gf[:], in_=gains[:])
-        quantize_x(0, 3)
+        for i in range(2):
+            nc.vector.tensor_tensor(out=gain_coef[:, i, :], in0=coefs[:, i, :], in1=gains[:], op=ALU.mult)
+        interleave_group("vector", 0, 2, 1)
+        quantize_x("vector", 0, 2)
+        quantize_x("vector", 0, 3)
         product(0, "q")
-        h_step(0)
-        h_step(1)
+        gain_h(0)
+        gain_h(1)
+        q_times_h(0)
 
-        def do(step, on_scalar):
-            kind = step[0]
-            if kind == "W":
-                widen(*step[1:], on_scalar)
-            elif kind == "I":
-                interleave_x(*step[1:], on_scalar)
-            elif kind == "Q":
-                quantize_x(*step[1:])
-            elif kind == "IZ":
-                interleave_z(*step[1:], on_scalar)
-            elif kind == "QZ":
-                quantize_z(*step[1:])
+        steps = {
+            "widen": widen,
+            "interleave_x": interleave_x,
+            "quantize_x": quantize_x,
+            "interleave_z": interleave_z,
+            "quantize_z": quantize_z,
+        }
 
-        for k in range(len(units)):
-            if k + 1 < len(units):
+        def take(table, k, engine):
+            for step in table.get(k, []):
+                steps[step[0]](engine, *step[1:])
+
+        for k in range(len(UNITS)):
+            if k + 1 < len(UNITS):
                 product(k + 1, "q")
-            if k + 2 < len(units):
+            if k + 2 < len(UNITS):
                 product(k + 2, "r")
             product(k, "p")
-            qh_step(k)
-            for s in PLAN["Va"].get(k, []):
-                do(s, False)
-            z_step(k)
-            for s in PLAN["Vb"].get(k, []):
-                do(s, False)
-            for s in PLAN["Sa"].get(k, []):
-                do(s, True)
-            if k + 2 < len(units):
-                h_step(k + 2)
-            for c, i, eng in PLAN["O"].get(k, []):
-                project(c, i, eng == "S")
-            for s in PLAN["Sb"].get(k, []):
-                do(s, True)
-        interleave_z(5, 0, 128, False)
-        quantize_z(5, 0, 128)
-        project_split(5, 0)
+            if k + 1 < len(UNITS):
+                q_times_h(k + 1)
+            take(VECTOR_BEFORE_Z, k, "vector")
+            make_z(k)
+            take(VECTOR_BEHIND_Z, k, "vector")
+            take(SCALAR_BEFORE_H, k, "scalar")
+            if k + 2 < len(UNITS):
+                gain_h(k + 2)
+            for c, tile_index, engine in PROJECTIONS.get(k, []):
+                project(c, tile_index, engine)
+            take(SCALAR_BEHIND_H, k, "scalar")
+
+        last = len(CHUNKS) - 1
+        interleave_z("vector", last, 0, P)
+        quantize_z("vector", last, 0, P)
+        project(last, 0, "vector", slice(0, E // 2))
+        project(last, 0, "scalar", slice(E // 2, E))

from contextlib import ExitStack

import concourse.mybir as mybir

F32 = mybir.dt.float32
BF16 = mybir.dt.bfloat16
I32 = mybir.dt.int32
U32 = mybir.dt.uint32
U8 = mybir.dt.uint8
FP8 = mybir.dt.float8_e4m3fn
FP8X4 = mybir.dt.float8_e4m3fn_x4

ALU = mybir.AluOpType
ACT = mybir.ActivationFunctionType

B, S, R, D, E = 2, 1024, 1024, 512, 512
P = 128
PACK = 4
K_PASS = P * PACK
GROUPS = S // K_PASS
BANK = 512
RUN = 4

FLOPS = 3 * 2 * B * R * S * D + 2 * B * R * D * E + 6 * B * R * D

CHUNKS = [(0, 0, 512), (0, 512, 512), (1, 0, 512), (1, 512, 256), (1, 768, 128), (1, 896, 128)]
UNITS = [(c, j) for c in range(len(CHUNKS)) for j in range(PACK)]

PLANE_START = {"r": 0, "q": 4, "p": 8, "o": 12}

WARM_UP = 9

VECTOR_BEFORE_Z = {
    2: [("widen", 1, 1, 1)],
    3: [("interleave_x", 1, 0)],
    4: [("quantize_x", 1, 0), ("quantize_x", 1, 1)],
    9: [("quantize_z", 1, 0, 256)],
    11: [("quantize_z", 1, 256, 512)],
    12: [("interleave_z", 2, 0, 256)],
    13: [("quantize_z", 2, 0, 256)],
}
VECTOR_BEHIND_Z = {
    0: [("widen", 1, 0, 3)],
    3: [("interleave_x", 1, 1)],
    6: [("quantize_x", 1, 2)],
    7: [("quantize_x", 1, 3), ("quantize_z", 0, 256, 512)],
    8: [("quantize_z", 0, 0, 256)],
    14: [("quantize_z", 2, 256, 512)],
    16: [("interleave_z", 3, 0, 256)],
    19: [("quantize_z", 3, 0, 256), ("interleave_z", 4, 0, 128)],
    20: [("quantize_z", 4, 0, 128)],
}
SCALAR_BEFORE_H = {
    0: [("widen", 1, 0, 2), ("widen", 1, 0, 1)],
    1: [("widen", 1, 0, 0)],
    3: [("interleave_x", 1, 3)],
    4: [("interleave_z", 0, 0, 256)],
    10: [("interleave_z", 1, 256, 512)],
    12: [("interleave_z", 2, 256, 512)],
}
SCALAR_BEHIND_H = {
    1: [("widen", 1, 1, 2)],
    2: [("widen", 1, 1, 3), ("widen", 1, 1, 0)],
    5: [("interleave_x", 1, 2)],
    6: [("interleave_z", 0, 256, 512)],
    7: [("interleave_z", 1, 0, 256)],
}
PROJECTIONS = {
    10: [(0, 2, "scalar"), (1, 0, "scalar")],
    11: [(0, 1, "scalar")],
    12: [(0, 3, "scalar"), (0, 0, "vector")],
    14: [(2, 0, "scalar"), (1, 2, "scalar")],
    15: [(1, 3, "scalar")],
    17: [(2, 1, "scalar")],
    18: [(1, 1, "scalar")],
    19: [(2, 2, "scalar")],
    20: [(3, 0, "scalar")],
    21: [(3, 1, "scalar")],
    23: [(4, 0, "scalar"), (2, 3, "scalar")],
}


def tile_volterrathirdordermixer_w8_kernel(
    tc,
    x_bytes,
    x_scale,
    mp_words,
    mp_scales,
    mq_words,
    mq_scales,
    mr_words,
    mr_scales,
    coef,
    gain,
    wo_words,
    wo_scales,
    out,
):
    nc = tc.nc
    words_in = {"r": mr_words, "q": mq_words, "p": mp_words}
    scales_in = {"r": mr_scales, "q": mq_scales, "p": mp_scales}

    with ExitStack() as ctx:
        keep = ctx.enter_context(tc.tile_pool(name="keep", bufs=1))
        work = ctx.enter_context(tc.tile_pool(name="work", bufs=3))
        psum = ctx.enter_context(tc.psum_pool(name="psum", bufs=2))
        ctx.enter_context(tc.manual_schedule())

        x_raw = [[keep.tile([P, PACK * D], U8, name="x_raw%d%d" % (b, g)) for g in range(GROUPS)] for b in range(B)]
        x_factor = keep.tile([P, GROUPS, PACK], F32, name="x_factor")
        x_wide = [keep.tile([P, GROUPS, PACK, D], BF16, name="x_wide%d" % b) for b in range(B)]
        x_mixed = [keep.tile([P, PACK, GROUPS, P * PACK], BF16, name="x_mixed%d" % b, align_bytes=64) for b in range(B)]
        x_codes = [keep.tile([P, PACK, GROUPS, P], U32, name="x_codes%d" % b, align_bytes=64) for b in range(B)]
        x_planes = [keep.tile([P, PACK, GROUPS, P], U8, name="x_planes%d" % b, align_bytes=64) for b in range(B)]

        m_codes = {
            (w, half): keep.tile([P, GROUPS, BANK], U32, name="m_codes_%s%d" % (w, half), align_bytes=64)
            for w in "rqp"
            for half in range(R // BANK)
        }
        m_planes = {w: keep.tile([P, GROUPS, R], U8, name="m_planes_" + w, align_bytes=64) for w in "rqp"}
        wo_codes = keep.tile([P, E], U32, name="wo_codes", align_bytes=64)
        wo_planes = keep.tile([P, E], U8, name="wo_planes", align_bytes=64)

        coefs = keep.tile([P, 2, PACK], BF16, name="coefs")
        gains = keep.tile([P, PACK], BF16, name="gains")
        gain_coef = keep.tile([P, 2, PACK], F32, name="gain_coef")
        zeros = keep.tile([P, BANK], BF16, name="zeros", align_bytes=64)
        first_act = keep.tile([P, 8], F32, name="first_act")

        def zero_plane(plane):
            nc.vector.memset(plane.bitcast(I32), 0)

        def load_x(b, g):
            rows = x_bytes[b, g * K_PASS : (g + 1) * K_PASS, :]
            nc.sync.dma_start(out=x_raw[b][g][:], in_=rows.rearrange("(p t) d -> p (t d)", t=PACK))

        def load_codes(w, half):
            view = words_in[w].rearrange("g p n t -> p g (n t)")
            cols = slice(half * BANK * PACK, (half + 1) * BANK * PACK)
            nc.sync.dma_start(out=m_codes[w, half][:].bitcast(I32), in_=view[:, :, cols].bitcast(I32))

        def load_scales(w):
            view = scales_in[w].rearrange("g (q i) n -> i q g n", i=4)
            for i in range(4):
                nc.sync.dma_start(out=m_planes[w][PLANE_START[w] + i : P : 32, :, :].bitcast(I32), in_=view[i].bitcast(I32))

        nc.gpsimd.memset(first_act[:], 0.0)
        nc.scalar.dma_start(out=x_factor[:], in_=x_scale[0].rearrange("(g p t) o -> p g (t o)", g=GROUPS, t=PACK))
        nc.gpsimd.dma_start(out=coefs[:], in_=coef.rearrange("c (p j) -> p c j", j=PACK))
        nc.gpsimd.dma_start(out=gains[:], in_=gain.rearrange("(p j) -> p j", j=PACK))
        nc.vector.memset(zeros[:], 0.0)
        for w in "rqp":
            zero_plane(m_planes[w][:].rearrange("p g n -> p (g n)"))
        zero_plane(wo_planes[:])

        load_x(0, 0)
        load_x(0, 1)
        load_scales("r")
        load_codes("r", 0)
        load_codes("q", 0)
        load_scales("q")
        load_codes("p", 0)
        load_scales("p")
        load_x(1, 0)
        load_x(1, 1)
        for w in "rqp":
            load_codes(w, 1)
        wo_view = wo_scales[0].rearrange("(q i) n -> i q n", i=4)
        for i in range(4):
            nc.sync.dma_start(out=wo_planes[PLANE_START["o"] + i : P : 32, :].bitcast(I32), in_=wo_view[i].bitcast(I32))
        nc.sync.dma_start(out=wo_codes[:].bitcast(I32), in_=wo_words[0].rearrange("p n t -> p (n t)").bitcast(I32))

        def copy(engine, dst, src):
            if engine == "scalar":
                nc.scalar.copy(out=dst, in_=src)
            else:
                nc.vector.tensor_copy(out=dst, in_=src)

        def widen(engine, b, g, t):
            src = x_raw[b][g][:, t * D : (t + 1) * D].bitcast(FP8)
            dst = x_wide[b][:, g, t, :]
            factor = x_factor[:, g, t : t + 1]
            if engine == "scalar":
                nc.scalar.activation(out=dst, in_=src, func=ACT.Copy, scale=factor)
            else:
                nc.vector.tensor_scalar(out=dst, in0=src, scalar1=factor, scalar2=None, op0=ALU.mult)

        def interleave_group(engine, b, j, g):
            src = x_wide[b][:, g].rearrange("p t (c i j) -> p j c t i", i=RUN, j=PACK)[:, j]
            dst = x_mixed[b][:, j, g].rearrange("p (c i t) -> p c t i", i=RUN, t=PACK)
            copy(engine, dst, src)

        def interleave_x(engine, b, j):
            for g in range(GROUPS):
                interleave_group(engine, b, j, g)

        def quantize_group(b, j, g):
            nc.vector.quantize_mx(out=x_codes[b][:, j, g].bitcast(FP8X4), scales=x_planes[b][:, j, g], in_=x_mixed[b][:, j, g])

        def quantize_x(engine, b, j):
            nc.vector.quantize_mx(
                out=x_codes[b][:, j].rearrange("p g m -> p (g m)").bitcast(FP8X4),
                scales=x_planes[b][:, j].rearrange("p g m -> p (g m)"),
                in_=x_mixed[b][:, j].rearrange("p g n -> p (g n)"),
            )

        banks, h_tiles, u_tiles = {}, {}, {}
        z_wide, z_mixed, z_codes, z_planes = {}, {}, {}, {}

        def product(k, w):
            c, j = UNITS[k]
            b, t0, n = CHUNKS[c]
            half, col = divmod(t0, BANK)
            bank = psum.tile([P, BANK], F32, name="bank_" + w)
            banks[k, w] = bank
            for g in range(GROUPS):
                nc.tensor.matmul_mx(
                    out=bank[:, :n],
                    lhsT=x_codes[b][:, j, g].bitcast(FP8X4),
                    lhsT_scale=x_planes[b][:, j, g],
                    rhs=m_codes[w, half][:, g, col : col + n].bitcast(FP8X4),
                    rhs_scale=m_planes[w][PLANE_START[w] : P, g, t0 : t0 + n],
                    start=(g == 0),
                    stop=(g == GROUPS - 1),
                )

        def gain_h(k):
            c, j = UNITS[k]
            n = CHUNKS[c][2]
            h = work.tile([P, BANK], F32, name="h")
            h_tiles[k] = h
            nc.scalar.activation(
                out=h[:, :n],
                in_=banks[k, "r"][:, :n],
                func=ACT.Identity,
                scale=gain_coef[:, 1, j : j + 1],
                bias=gain_coef[:, 0, j : j + 1],
            )

        def q_times_h(k):
            n = CHUNKS[UNITS[k][0]][2]
            u = work.tile([P, BANK], F32, name="u")
            u_tiles[k] = u
            nc.vector.tensor_tensor(out=u[:, :n], in0=banks[k, "q"][:, :n], in1=h_tiles[k][:, :n], op=ALU.mult)

        def make_z(k):
            c, j = UNITS[k]
            n = CHUNKS[c][2]
            if j == 0:
                z_wide[c] = work.tile([P, PACK, BANK], BF16, name="z_wide")
            nc.vector.scalar_tensor_tensor(
                out=z_wide[c][:, j, :n],
                in0=u_tiles[k][:, :n],
                scalar=gains[:, j : j + 1],
                in1=banks[k, "p"][:, :n],
                op0=ALU.add,
                op1=ALU.mult,
            )

        def interleave_z(engine, c, lo, hi):
            if c not in z_mixed:
                z_mixed[c] = work.tile([P, BANK, PACK], BF16, name="z_mixed", align_bytes=64)
            src = z_wide[c][:, :, lo:hi].rearrange("p j (c i) -> p c j i", i=RUN)
            dst = z_mixed[c][:, lo:hi, :].rearrange("p (c i) j -> p c j i", i=RUN)
            copy(engine, dst, src)

        def quantize_z(engine, c, lo, hi):
            if c not in z_codes:
                z_codes[c] = work.tile([P, BANK], U32, name="z_codes", align_bytes=64)
                z_planes[c] = work.tile([P, BANK], U8, name="z_planes", align_bytes=64)
            nc.vector.quantize_mx(
                out=z_codes[c][:, lo:hi].bitcast(FP8X4),
                scales=z_planes[c][:, lo:hi],
                in_=z_mixed[c][:, lo:hi, :].rearrange("p t j -> p (t j)"),
            )

        def project(c, tile_index, engine, cols=slice(0, E)):
            b, t0, n = CHUNKS[c]
            width = cols.stop - cols.start
            times = slice(tile_index * P, (tile_index + 1) * P)
            bank = psum.tile([P, BANK], F32, name="bank_o")
            nc.tensor.matmul_mx(
                out=bank[:, :width],
                lhsT=z_codes[c][:, times].bitcast(FP8X4),
                lhsT_scale=z_planes[c][:, times],
                rhs=wo_codes[:, cols].bitcast(FP8X4),
                rhs_scale=wo_planes[PLANE_START["o"] : P, cols],
                start=True,
                stop=True,
            )
            result = work.tile([P, E], F32, name="result", bufs=6)
            copy(engine, result[:, :width], bank[:, :width])
            nc.sync.dma_start(out=out[b, t0 + times.start : t0 + times.stop, cols], in_=result[:, :width])

        idle = psum.tile([P, BANK], F32, name="bank_o")
        for i in range(WARM_UP):
            nc.tensor.matmul(out=idle[:], lhsT=zeros[:, :P], rhs=zeros[:], start=True, stop=True)
        nc.scalar.activation(out=first_act[:, 4:5], in_=first_act[:, 0:1], func=ACT.Identity)
        for g in range(GROUPS):
            for t in range(PACK):
                widen("vector" if t < 3 - g else "scalar", 0, g, t)
        interleave_group("vector", 0, 0, 0)
        interleave_group("scalar", 0, 0, 1)
        quantize_group(0, 0, 0)
        interleave_group("vector", 0, 1, 0)
        quantize_group(0, 0, 1)
        interleave_group("vector", 0, 1, 1)
        product(0, "r")
        interleave_x("scalar", 0, 3)
        quantize_group(0, 1, 0)
        interleave_group("vector", 0, 2, 0)
        quantize_group(0, 1, 1)
        product(1, "r")
        for i in range(2):
            nc.vector.tensor_tensor(out=gain_coef[:, i, :], in0=coefs[:, i, :], in1=gains[:], op=ALU.mult)
        interleave_group("vector", 0, 2, 1)
        quantize_x("vector", 0, 2)
        quantize_x("vector", 0, 3)
        product(0, "q")
        gain_h(0)
        gain_h(1)
        q_times_h(0)

        steps = {
            "widen": widen,
            "interleave_x": interleave_x,
            "quantize_x": quantize_x,
            "interleave_z": interleave_z,
            "quantize_z": quantize_z,
        }

        def take(table, k, engine):
            for step in table.get(k, []):
                steps[step[0]](engine, *step[1:])

        for k in range(len(UNITS)):
            if k + 1 < len(UNITS):
                product(k + 1, "q")
            if k + 2 < len(UNITS):
                product(k + 2, "r")
            product(k, "p")
            if k + 1 < len(UNITS):
                q_times_h(k + 1)
            take(VECTOR_BEFORE_Z, k, "vector")
            make_z(k)
            take(VECTOR_BEHIND_Z, k, "vector")
            take(SCALAR_BEFORE_H, k, "scalar")
            if k + 2 < len(UNITS):
                gain_h(k + 2)
            for c, tile_index, engine in PROJECTIONS.get(k, []):
                project(c, tile_index, engine)
            take(SCALAR_BEHIND_H, k, "scalar")

        last = len(CHUNKS) - 1
        interleave_z("vector", last, 0, P)
        quantize_z("vector", last, 0, P)
        project(last, 0, "vector", slice(0, E // 2))
        project(last, 0, "scalar", slice(E // 2, E))
